import numpy as np
import ml_dtypes


def mxq(x, axis, fmt="e4m3"):
    dtype, down = {"e4m3": (ml_dtypes.float8_e4m3fn, 7), "e5m2": (ml_dtypes.float8_e5m2, 14)}[fmt]
    v = np.moveaxis(np.asarray(x, np.float32).astype(ml_dtypes.bfloat16).astype(np.float64), axis, -1)
    blocks = v.reshape(v.shape[:-1] + (-1, 32))
    amax = np.abs(blocks).max(-1, keepdims=True)
    byte = np.maximum(np.where(amax > 0, np.frexp(amax)[1] - 1 + 127, 0) - down, 1)
    scale = np.exp2(byte - 127.0)
    codes = (blocks / scale).astype(np.float32).astype(dtype).astype(np.float64)
    return np.moveaxis((codes * scale).reshape(v.shape), -1, axis)


WIDE = False


def mx_kscale(k):
    if not WIDE:
        return np.ones(k)
    levels = np.array([10, -10, 5, -5, 0])
    if k % 512:
        return np.exp2(np.random.permutation(np.resize(levels, k // 32))).repeat(32)
    a = np.empty((k // 512, 16))
    for p in range(k // 512):
        a[p, :8] = np.random.permutation(np.resize(levels, 8))
        for g in range(8):
            far = levels[np.abs(levels - a[p, g]) >= 10]
            a[p, g + 8] = far[np.random.randint(len(far))]
    return np.exp2(a.ravel()).repeat(32)


def f64(x):
    return np.asarray(x).astype(np.float64)


def striped(idx):
    return np.tile(idx.reshape(-1, 16).T, (8, 1)).astype(np.uint16)


def unstriped(offs):
    return offs[:16].T.reshape(-1).astype(np.int64)


def striped8(idx):
    return np.concatenate([x.reshape(-1, 16).T for x in idx]).astype(np.uint16)


def runs(offs, k):
    lists = np.stack([offs[16 * r : 16 * r + 16].T.reshape(-1) for r in range(8)]).astype(np.int64)
    return lists[np.arange(k) % 512 // 64]


def pack_weight(w):
    k, n = w.shape
    w = f64(np.asarray(w, np.float32).astype(ml_dtypes.bfloat16)).reshape(k // 32, 32, n)
    amax = np.abs(w).max(1)
    byte = np.clip(np.where(amax > 0, np.frexp(amax)[1] - 1 + 127 - 7, 1), 1, 254)
    scaled = (w * np.exp2(127.0 - byte)[:, None, :]).reshape(k, n).astype(np.float32)
    words = np.ascontiguousarray(scaled.reshape(k // 512, 128, 4, n).transpose(0, 1, 3, 2)).astype(ml_dtypes.float8_e4m3fn).view(np.uint8)
    return words, np.ascontiguousarray(byte.astype(np.uint8).reshape(k // 512, 16, n))


def unpack_weight(words, scales):
    g, p, n, _ = words.shape
    vals = np.ascontiguousarray(words).view(ml_dtypes.float8_e4m3fn).astype(np.float64) * np.repeat(np.exp2(scales.astype(np.float64) - 127.0), 8, axis=1)[..., None]
    return vals.transpose(0, 1, 3, 2).reshape(g * 512, n)


def relu(v):
    return np.maximum(v, 0.0)


K, T, S, V, H, W = 512, 2048, 512, 512, 512, 256


def setup_inputs():
    n = np.random.standard_normal
    s = mx_kscale(K)[:, None]
    u = mx_kscale(S)
    packed_xT = pack_weight(n((K, T)) * s)
    perm = np.stack([np.random.permutation(S) for _ in range(8)])
    return {
        "x_words": packed_xT[0],
        "x_scales": packed_xT[1],
        "w1": (n((K, H)) / np.sqrt(K) / s).astype(np.float32),
        "w2": (n((K, H)) / np.sqrt(K) / s).astype(np.float32),
        "ga": (np.random.uniform(0.5, 1.5, (H, 1)) * u[:, None]).astype(np.float32),
        "gb": (np.random.uniform(0.5, 1.5, (H, 1)) / u[:, None]).astype(np.float32),
        "offs": striped(np.random.permutation(T)[:S]),
        "two": striped(np.random.permutation(T)[:V]),
        "la": striped8(perm[:, :W]),
        "lb": striped8(perm[:, W:]),
        "nq": striped8(np.stack([np.random.permutation(V) for _ in range(8)])),
    }


def reference(x_words, x_scales, w1, w2, ga, gb, offs, two, la, lb, nq):
    xq = unpack_weight(x_words, x_scales)[:, unstriped(offs)]
    a = mxq(f64(w1), 0, "e4m3").T @ xq
    p = a[np.arange(H)[:, None], runs(la, H)]
    qv = a[np.arange(H)[:, None], runs(lb, H)]
    lo = np.minimum(p, qv)
    hi = np.maximum(p, qv)
    d1 = np.zeros((H, S))
    d1[np.arange(H)[:, None], runs(la, H)] = hi
    d2 = d1.copy()
    d2[np.arange(H)[:, None], runs(lb, H)] = lo
    z = f64(ga) * d2
    x_two = unpack_weight(x_words, x_scales)[:, unstriped(two)]
    b = mxq(f64(w2), 0, "e4m3").T @ x_two
    z2 = f64(gb) * (b[np.arange(H)[:, None], runs(nq, H)])
    s = 0.0625 * ((mxq(z, 0, "e4m3").T @ mxq(z2, 0, "e4m3")))
    return relu(s)

@@ -1,0 +1,217 @@
+from contextlib import ExitStack
+
+import concourse.mybir as mybir
+
+K, T, S, V, H, W = 512, 2048, 512, 512, 512, 256
+FLOPS = 2 * K * H * S + 2 * K * H * V + 2 * H * S * V
+
+F32 = mybir.dt.float32
+BF16 = mybir.dt.bfloat16
+I32 = mybir.dt.int32
+U32 = mybir.dt.uint32
+U16 = mybir.dt.uint16
+U8 = mybir.dt.uint8
+FP8X4 = mybir.dt.float8_e4m3fn_x4
+ALU = mybir.AluOpType
+ACT = mybir.ActivationFunctionType
+
+P = 128
+PACK = 4
+PER_COL = 16
+CHUNKS = (256, 128, 128)
+
+
+def tile_picked_keyord_none_p_kernel(
+    tc, x_words, x_scales, w1, w2, ga, gb, offs, two, la, lb, nq, out
+):
+    nc = tc.nc
+    with ExitStack() as ctx:
+        keep = ctx.enter_context(tc.tile_pool(name="keep", bufs=1))
+        psum = ctx.enter_context(tc.psum_pool(name="psum", bufs=8))
+
+        def sb(shape, dtype, name, tag=None):
+            return keep.tile(shape, dtype, name=name, tag=tag or name, align_bytes=64)
+
+        def load_list(src, name):
+            tile = sb([P, src.shape[1]], U16, name)
+            nc.sync.dma_start(tile[:], src)
+            return tile
+
+        def mx(acc, lhs, lhs_cols, rhs, rhs_cols):
+            nc.tensor.matmul_mx(
+                out=acc,
+                lhsT=lhs[0][:, lhs_cols].bitcast(FP8X4),
+                lhsT_scale=lhs[1][:, lhs_cols],
+                rhs=rhs[0][:, rhs_cols].bitcast(FP8X4),
+                rhs_scale=rhs[1][:, rhs_cols],
+                start=True,
+                stop=True,
+            )
+
+        def quantize(src, cols, name):
+            codes = sb([P, cols], U32, name + "_codes")
+            scales = sb([P, cols], U8, name + "_scales")
+            nc.vector.quantize_mx(out=codes[:].bitcast(FP8X4), scales=scales[:], in_=src)
+            return codes, scales
+
+        table_scales = sb([P, T], U8, "table_scales")
+        nc.vector.memset(table_scales[:].bitcast(I32), 0)
+        offs_t = load_list(offs, "offs_t")
+        two_t = load_list(two, "two_t")
+        w1_raw = sb([P, PACK, H], F32, "w1_raw")
+        w1_v = w1.rearrange("(p j) c -> p j c", j=PACK)
+        nc.sync.dma_start(w1_raw[:, 0:2, :], w1_v[:, 0:2, :])
+        for q in range(4):
+            nc.sync.dma_start(
+                table_scales[32 * q : 32 * q + 4, :].bitcast(I32),
+                x_scales[0, 4 * q : 4 * q + 4, :].bitcast(I32),
+            )
+        nc.sync.dma_start(w1_raw[:, 2:4, :], w1_v[:, 2:4, :])
+        table_words = sb([P, T], U32, "table_words")
+        nc.sync.dma_start(
+            table_words[:].bitcast(I32), x_words[0].rearrange("p n t -> p (n t)").bitcast(I32)
+        )
+        la_t = load_list(la, "la_t")
+        lb_t = load_list(lb, "lb_t")
+        w2_raw = sb([P, PACK, H], F32, "w2_raw")
+        nc.sync.dma_start(w2_raw[:], w2.rearrange("(p j) c -> p j c", j=PACK))
+        ga_t = sb([P, PACK], F32, "ga_t")
+        nc.sync.dma_start(ga_t[:], ga.rearrange("(p t) o -> p (t o)", t=PACK))
+        gb_t = sb([P, PACK], F32, "gb_t")
+        nc.sync.dma_start(gb_t[:], gb.rearrange("(p t) o -> p (t o)", t=PACK))
+        nq_t = load_list(nq, "nq_t")
+
+        def cast_pair(raw, u, name, copy=nc.scalar.copy):
+            grouped = sb([P, 2, P, PACK], BF16, name)
+            copy(
+                grouped[:].rearrange("p t m j -> p m j t"),
+                raw[:].rearrange("p j (m t) -> p m j t", t=PACK)[:, :, :, 2 * u : 2 * u + 2],
+            )
+            return grouped
+
+        def quantize_pair(grouped, name):
+            return quantize(grouped[:].rearrange("p t m j -> p (t m j)"), 2 * P, name)
+
+        xa_scales = sb([P, S], U8, "xa_scales")
+        xb_scales = sb([P, V], U8, "xb_scales")
+        xa_words = sb([P, S], U32, "xa_words")
+        xb_words = sb([P, V], U32, "xb_words")
+        nc.vector.tensor_copy(xa_scales[:], table_scales[:].indirect(offs_t[:]))
+        w1_q = []
+        for u in range(2):
+            w1_q.append(quantize_pair(cast_pair(w1_raw, u, "w1_bf%d" % u, nc.scalar.copy if u else nc.vector.tensor_copy), "w1_%d" % u))
+        nc.vector.tensor_copy(xb_scales[:], table_scales[:].indirect(two_t[:]))
+        half = S // 2
+        for h in range(2):
+            nc.vector.tensor_copy(
+                xa_words[:, h * half : (h + 1) * half],
+                table_words[:].indirect(offs_t[:, h * half // PER_COL : (h + 1) * half // PER_COL]),
+            )
+        xa = (xa_words, xa_scales)
+        xb = (xb_words, xb_scales)
+
+        a_rows = []
+        for t in range(PACK):
+            rows = sb([P, S], F32, "a%d" % t)
+            cols = slice((t % 2) * P, (t % 2 + 1) * P)
+            pieces = 2 if t == 0 else 1
+            width = S // pieces
+            for h in range(pieces):
+                acc = psum.tile([P, width], F32, name="acc", tag="bank")
+                span = slice(h * width, (h + 1) * width)
+                mx(acc[:], w1_q[t // 2], cols, xa, span)
+                nc.scalar.copy(rows[:, span], acc[:])
+            a_rows.append(rows)
+        nc.vector.tensor_copy(xb_words[:], table_words[:].indirect(two_t[:]))
+
+        w2_bf = sb([P, PACK, P, PACK], BF16, "w2_bf")
+        nc.scalar.copy(
+            w2_bf[:].rearrange("p t m j -> p m j t"),
+            w2_raw[:].rearrange("p j (m t) -> p m j t", t=PACK),
+        )
+
+        z_bf = sb([P, S, PACK], BF16, "z_bf", "w2_raw")
+        sorted_rows = []
+
+        def order_pairs(t, pair):
+            pq = pair[:, t % 2]
+            nc.vector.tensor_copy(pq[:, 0, :], a_rows[t][:].indirect(la_t[:]))
+            nc.vector.tensor_copy(pq[:, 1, :], a_rows[t][:].indirect(lb_t[:]))
+            hi = sb([P, W], F32, "hi%d" % t)
+            lo = sb([P, W], F32, "lo%d" % t)
+            nc.vector.tensor_tensor(hi[:], pq[:, 0, :], pq[:, 1, :], ALU.max)
+            nc.vector.tensor_tensor(lo[:], pq[:, 0, :], pq[:, 1, :], ALU.min)
+            d = sb([P, S], F32, "d%d" % t)
+            nc.vector.tensor_copy(d[:].indirect(la_t[:]), hi[:])
+            nc.vector.tensor_copy(d[:].indirect(lb_t[:]), lo[:])
+            sorted_rows.append(d)
+
+        def weave_z(t):
+            nc.scalar.activation(
+                z_bf[:, :, t], sorted_rows[t][:], ACT.Copy, scale=ga_t[:, t : t + 1]
+            )
+
+        pq01 = sb([P, 2, 2, W], F32, "pq01")
+        order_pairs(0, pq01)
+        weave_z(0)
+        order_pairs(1, pq01)
+        w2_q = quantize(w2_bf[:].rearrange("p t m j -> p (t m j)"), H, "w2")
+        weave_z(1)
+        b_rows = []
+        for t in range(PACK):
+            rows = sb([P, V], F32, "b%d" % t)
+            acc = psum.tile([P, V], F32, name="acc", tag="bank")
+            mx(acc[:], w2_q, slice(t * P, (t + 1) * P), xb, slice(0, V))
+            nc.scalar.activation(rows[:], acc[:], ACT.Copy, scale=gb_t[:, t : t + 1])
+            b_rows.append(rows)
+        pq23 = sb([P, 2, 2, W], F32, "pq23", "w2_bf")
+        order_pairs(2, pq23)
+        weave_z(2)
+        order_pairs(3, pq23)
+        weave_z(3)
+
+        out_v = out.rearrange("(m p) v -> p m v", p=P)
+        gates = ("hi3", "w2_raw", "z2_bf0")
+        starts = [sum(CHUNKS[:c]) for c in range(len(CHUNKS))]
+        z2_bf = []
+
+        def fetch(c):
+            n = CHUNKS[c]
+            planes = sb([P, PACK, n], BF16, "planes%d" % c, gates[c])
+            lst = nq_t[:, starts[c] // PER_COL : (starts[c] + n) // PER_COL]
+            for t in range(PACK):
+                nc.vector.tensor_copy(planes[:, t, :], b_rows[t][:].indirect(lst))
+            woven = sb([P, n, PACK], BF16, "z2_bf%d" % c)
+            src = planes[:].rearrange("p t n -> p n t")
+            if c == len(CHUNKS) - 1:
+                nc.vector.tensor_copy(woven[:], src)
+            else:
+                nc.scalar.copy(woven[:], src)
+            z2_bf.append(woven)
+
+        def finish(c, z_q):
+            n = CHUNKS[c]
+            z2_q = quantize(z2_bf[c][:].rearrange("p n t -> p (n t)"), n, "z2_%d" % c)
+            last = c == len(CHUNKS) - 1
+            per_bank = 2 if (last or n == 256) else 4
+            for g in range(PACK // per_bank):
+                acc = psum.tile([P, per_bank, n], F32, name="acc", tag="bank")
+                for i in range(per_bank):
+                    m = g * per_bank + i
+                    mx(acc[:, i, :], z_q, slice(m * P, (m + 1) * P), z2_q, slice(0, n))
+                res = sb([P, per_bank, n], F32, "res%d_%d" % (c, g))
+                if last and g == 1:
+                    nc.vector.tensor_scalar(res[:], acc[:], 0.0625, 0.0, ALU.mult, ALU.max)
+                else:
+                    nc.scalar.activation(res[:], acc[:], ACT.Relu, scale=0.0625)
+                nc.sync.dma_start(
+                    out_v[:, g * per_bank : (g + 1) * per_bank, starts[c] : starts[c] + n], res[:]
+                )
+
+        fetch(0)
+        z_q = quantize(z_bf[:].rearrange("p n t -> p (n t)"), S, "z")
+        fetch(1)
+        finish(0, z_q)
+        fetch(2)
+        finish(1, z_q)
+        finish(2, z_q)

@@ -27,6 +27,7 @@ def tile_picked_keyord_none_p_kernel(
     nc = tc.nc
     with ExitStack() as ctx:
         keep = ctx.enter_context(tc.tile_pool(name="keep", bufs=1))
+        reuse = ctx.enter_context(tc.tile_pool(name="reuse", bufs=1))
         psum = ctx.enter_context(tc.psum_pool(name="psum", bufs=8))
 
         def sb(shape, dtype, name, tag=None):
@@ -63,8 +64,8 @@ def tile_picked_keyord_none_p_kernel(
         nc.sync.dma_start(w1_raw[:, 0:2, :], w1_v[:, 0:2, :])
         for q in range(4):
             nc.sync.dma_start(
-                table_scales[32 * q : 32 * q + 4, :].bitcast(I32),
-                x_scales[0, 4 * q : 4 * q + 4, :].bitcast(I32),
+                table_scales[q:P:32, :].bitcast(I32),
+                x_scales[0, q:16:4, :].bitcast(I32),
             )
         nc.sync.dma_start(w1_raw[:, 2:4, :], w1_v[:, 2:4, :])
         table_words = sb([P, T], U32, "table_words")
@@ -73,7 +74,7 @@ def tile_picked_keyord_none_p_kernel(
         )
         la_t = load_list(la, "la_t")
         lb_t = load_list(lb, "lb_t")
-        w2_raw = sb([P, PACK, H], F32, "w2_raw")
+        w2_raw = reuse.tile([P, PACK, H], F32, name="w2_raw", align_bytes=64, offset=0)
         nc.sync.dma_start(w2_raw[:], w2.rearrange("(p j) c -> p j c", j=PACK))
         ga_t = sb([P, PACK], F32, "ga_t")
         nc.sync.dma_start(ga_t[:], ga.rearrange("(p t) o -> p (t o)", t=PACK))
@@ -130,7 +131,7 @@ def tile_picked_keyord_none_p_kernel(
             w2_raw[:].rearrange("p j (m t) -> p m j t", t=PACK),
         )
 
-        z_bf = sb([P, S, PACK], BF16, "z_bf", "w2_raw")
+        z_bf = reuse.tile([P, S, PACK], BF16, name="z_bf", align_bytes=64, offset=0)
         sorted_rows = []
 
         def order_pairs(t, pair):
@@ -164,14 +165,14 @@ def tile_picked_keyord_none_p_kernel(
             mx(acc[:], w2_q, slice(t * P, (t + 1) * P), xb, slice(0, V))
             nc.scalar.activation(rows[:], acc[:], ACT.Copy, scale=gb_t[:, t : t + 1])
             b_rows.append(rows)
-        pq23 = sb([P, 2, 2, W], F32, "pq23", "w2_bf")
+        pq23 = reuse.tile([P, 2, 2, W], F32, name="pq23", align_bytes=64, offset=4096)
         order_pairs(2, pq23)
         weave_z(2)
         order_pairs(3, pq23)
         weave_z(3)
 
         out_v = out.rearrange("(m p) v -> p m v", p=P)
-        gates = ("hi3", "w2_raw", "z2_bf0")
+        gates = ("hi3", "d3", "hi3")
         starts = [sum(CHUNKS[:c]) for c in range(len(CHUNKS))]
         z2_bf = []
 
@@ -200,11 +201,12 @@ def tile_picked_keyord_none_p_kernel(
                     m = g * per_bank + i
                     mx(acc[:, i, :], z_q, slice(m * P, (m + 1) * P), z2_q, slice(0, n))
                 res = sb([P, per_bank, n], F32, "res%d_%d" % (c, g))
-                if last and g == 1:
+                if last:
                     nc.vector.tensor_scalar(res[:], acc[:], 0.0625, 0.0, ALU.mult, ALU.max)
                 else:
                     nc.scalar.activation(res[:], acc[:], ACT.Relu, scale=0.0625)
-                nc.sync.dma_start(
+                queue = nc.scalar if c == 1 else nc.sync
+                queue.dma_start(
                     out_v[:, g * per_bank : (g + 1) * per_bank, starts[c] : starts[c] + n], res[:]
                 )
 

@@ -19,6 +19,9 @@ P = 128
 PACK = 4
 PER_COL = 16
 CHUNKS = (256, 128, 128)
+CODES_AT = 9216
+HI_AT = {2: 4096, 3: 5120}
+LO_AT = {2: 7168, 3: 6144}
 
 
 def tile_picked_keyord_none_p_kernel(
@@ -49,25 +52,31 @@ def tile_picked_keyord_none_p_kernel(
                 stop=True,
             )
 
-        def quantize(src, cols, name):
-            codes = sb([P, cols], U32, name + "_codes")
+        def quantize(src, cols, name, at=None):
+            if at is None:
+                codes = sb([P, cols], U32, name + "_codes")
+            else:
+                codes = reuse.tile([P, cols], U32, name=name + "_codes", align_bytes=64, offset=at)
             scales = sb([P, cols], U8, name + "_scales")
             nc.vector.quantize_mx(out=codes[:].bitcast(FP8X4), scales=scales[:], in_=src)
             return codes, scales
 
         table_scales = sb([P, T], U8, "table_scales")
         nc.vector.memset(table_scales[:].bitcast(I32), 0)
+        warm = sb([P, 2], F32, "warm")
+        nc.vector.memset(warm[:, 0:1], 0.0)
+        nc.scalar.activation(warm[:, 1:2], warm[:, 0:1], ACT.Relu)
         offs_t = load_list(offs, "offs_t")
         two_t = load_list(two, "two_t")
         w1_raw = sb([P, PACK, H], F32, "w1_raw")
         w1_v = w1.rearrange("(p j) c -> p j c", j=PACK)
-        nc.sync.dma_start(w1_raw[:, 0:2, :], w1_v[:, 0:2, :])
+        nc.sync.dma_start(w1_raw[:, 0:1, :], w1_v[:, 0:1, :])
         for q in range(4):
             nc.sync.dma_start(
                 table_scales[q:P:32, :].bitcast(I32),
                 x_scales[0, q:16:4, :].bitcast(I32),
             )
-        nc.sync.dma_start(w1_raw[:, 2:4, :], w1_v[:, 2:4, :])
+        nc.sync.dma_start(w1_raw[:, 1:4, :], w1_v[:, 1:4, :])
         table_words = sb([P, T], U32, "table_words")
         nc.sync.dma_start(
             table_words[:].bitcast(I32), x_words[0].rearrange("p n t -> p (n t)").bitcast(I32)
@@ -90,18 +99,17 @@ def tile_picked_keyord_none_p_kernel(
             )
             return grouped
 
-        def quantize_pair(grouped, name):
-            return quantize(grouped[:].rearrange("p t m j -> p (t m j)"), 2 * P, name)
-
         xa_scales = sb([P, S], U8, "xa_scales")
         xb_scales = sb([P, V], U8, "xb_scales")
         xa_words = sb([P, S], U32, "xa_words")
         xb_words = sb([P, V], U32, "xb_words")
         nc.vector.tensor_copy(xa_scales[:], table_scales[:].indirect(offs_t[:]))
-        w1_q = []
-        for u in range(2):
-            w1_q.append(quantize_pair(cast_pair(w1_raw, u, "w1_bf%d" % u, nc.scalar.copy if u else nc.vector.tensor_copy), "w1_%d" % u))
         nc.vector.tensor_copy(xb_scales[:], table_scales[:].indirect(two_t[:]))
+        w1_bf = [cast_pair(w1_raw, u, "w1_bf%d" % u) for u in range(2)]
+        w1_q = [
+            quantize(w1_bf[0][:, t].rearrange("p m j -> p (m j)"), P, "w1_%d" % t, CODES_AT if t == 0 else None)
+            for t in range(2)
+        ]
         half = S // 2
         for h in range(2):
             nc.vector.tensor_copy(
@@ -114,16 +122,18 @@ def tile_picked_keyord_none_p_kernel(
         a_rows = []
         for t in range(PACK):
             rows = sb([P, S], F32, "a%d" % t)
-            cols = slice((t % 2) * P, (t % 2 + 1) * P)
+            if t == 2:
+                nc.vector.tensor_copy(xb_words[:], table_words[:].indirect(two_t[:]))
+                w1_q.append(quantize(w1_bf[1][:].rearrange("p t m j -> p (t m j)"), 2 * P, "w1_23", CODES_AT))
+            cols = slice(P, 2 * P) if t == 3 else slice(0, P)
             pieces = 2 if t == 0 else 1
             width = S // pieces
             for h in range(pieces):
                 acc = psum.tile([P, width], F32, name="acc", tag="bank")
                 span = slice(h * width, (h + 1) * width)
-                mx(acc[:], w1_q[t // 2], cols, xa, span)
+                mx(acc[:], w1_q[min(t, 2)], cols, xa, span)
                 nc.scalar.copy(rows[:, span], acc[:])
             a_rows.append(rows)
-        nc.vector.tensor_copy(xb_words[:], table_words[:].indirect(two_t[:]))
 
         w2_bf = sb([P, PACK, P, PACK], BF16, "w2_bf")
         nc.scalar.copy(
@@ -138,8 +148,12 @@ def tile_picked_keyord_none_p_kernel(
             pq = pair[:, t % 2]
             nc.vector.tensor_copy(pq[:, 0, :], a_rows[t][:].indirect(la_t[:]))
             nc.vector.tensor_copy(pq[:, 1, :], a_rows[t][:].indirect(lb_t[:]))
-            hi = sb([P, W], F32, "hi%d" % t)
-            lo = sb([P, W], F32, "lo%d" % t)
+            if t < 2:
+                hi = sb([P, W], F32, "hi%d" % t)
+                lo = sb([P, W], F32, "lo%d" % t)
+            else:
+                hi = reuse.tile([P, W], F32, name="hi%d" % t, align_bytes=64, offset=HI_AT[t])
+                lo = reuse.tile([P, W], F32, name="lo%d" % t, align_bytes=64, offset=LO_AT[t])
             nc.vector.tensor_tensor(hi[:], pq[:, 0, :], pq[:, 1, :], ALU.max)
             nc.vector.tensor_tensor(lo[:], pq[:, 0, :], pq[:, 1, :], ALU.min)
             d = sb([P, S], F32, "d%d" % t)
@@ -148,9 +162,12 @@ def tile_picked_keyord_none_p_kernel(
             sorted_rows.append(d)
 
         def weave_z(t):
-            nc.scalar.activation(
-                z_bf[:, :, t], sorted_rows[t][:], ACT.Copy, scale=ga_t[:, t : t + 1]
-            )
+            pieces = 2 if t == PACK - 1 else 1
+            for h in range(pieces):
+                span = slice(h * S // pieces, (h + 1) * S // pieces)
+                nc.scalar.activation(
+                    z_bf[:, span, t], sorted_rows[t][:, span], ACT.Copy, scale=ga_t[:, t : t + 1]
+                )
 
         pq01 = sb([P, 2, 2, W], F32, "pq01")
         order_pairs(0, pq01)
@@ -165,20 +182,22 @@ def tile_picked_keyord_none_p_kernel(
             mx(acc[:], w2_q, slice(t * P, (t + 1) * P), xb, slice(0, V))
             nc.scalar.activation(rows[:], acc[:], ACT.Copy, scale=gb_t[:, t : t + 1])
             b_rows.append(rows)
-        pq23 = reuse.tile([P, 2, 2, W], F32, name="pq23", align_bytes=64, offset=4096)
+        pq23 = sb([P, 2, 2, W], F32, "pq23")
         order_pairs(2, pq23)
         weave_z(2)
         order_pairs(3, pq23)
         weave_z(3)
 
         out_v = out.rearrange("(m p) v -> p m v", p=P)
-        gates = ("hi3", "d3", "hi3")
         starts = [sum(CHUNKS[:c]) for c in range(len(CHUNKS))]
         z2_bf = []
 
         def fetch(c):
             n = CHUNKS[c]
-            planes = sb([P, PACK, n], BF16, "planes%d" % c, gates[c])
+            if c == 1:
+                planes = sb([P, PACK, n], BF16, "planes1", "d3")
+            else:
+                planes = reuse.tile([P, PACK, n], BF16, name="planes%d" % c, align_bytes=64, offset=LO_AT[2])
             lst = nq_t[:, starts[c] // PER_COL : (starts[c] + n) // PER_COL]
             for t in range(PACK):
                 nc.vector.tensor_copy(planes[:, t, :], b_rows[t][:].indirect(lst))
@@ -199,7 +218,7 @@ def tile_picked_keyord_none_p_kernel(
                 acc = psum.tile([P, per_bank, n], F32, name="acc", tag="bank")
                 for i in range(per_bank):
                     m = g * per_bank + i
-                    mx(acc[:, i, :], z_q, slice(m * P, (m + 1) * P), z2_q, slice(0, n))
+                    mx(acc[:, i, :], z_q[m // 2], slice(m % 2 * P, (m % 2 + 1) * P), z2_q, slice(0, n))
                 res = sb([P, per_bank, n], F32, "res%d_%d" % (c, g))
                 if last:
                     nc.vector.tensor_scalar(res[:], acc[:], 0.0625, 0.0, ALU.mult, ALU.max)
@@ -211,7 +230,10 @@ def tile_picked_keyord_none_p_kernel(
                 )
 
         fetch(0)
-        z_q = quantize(z_bf[:].rearrange("p n t -> p (n t)"), S, "z")
+        z_q = [
+            quantize(z_bf[:, h * half : (h + 1) * half, :].rearrange("p n t -> p (n t)"), half, "z_%d" % h)
+            for h in range(2)
+        ]
         fetch(1)
         finish(0, z_q)
         fetch(2)

from contextlib import ExitStack

import concourse.mybir as mybir

K, T, S, V, H, W = 512, 2048, 512, 512, 512, 256
FLOPS = 2 * K * H * S + 2 * K * H * V + 2 * H * S * V

F32 = mybir.dt.float32
BF16 = mybir.dt.bfloat16
I32 = mybir.dt.int32
U32 = mybir.dt.uint32
U16 = mybir.dt.uint16
U8 = mybir.dt.uint8
FP8X4 = mybir.dt.float8_e4m3fn_x4
ALU = mybir.AluOpType
ACT = mybir.ActivationFunctionType

P = 128
PACK = 4
PER_COL = 16
CHUNKS = (256, 128, 128)
CODES_AT = 9216
HI_AT = {2: 4096, 3: 5120}
LO_AT = {2: 7168, 3: 6144}


def tile_picked_keyord_none_p_kernel(
    tc, x_words, x_scales, w1, w2, ga, gb, offs, two, la, lb, nq, out
):
    nc = tc.nc
    with ExitStack() as ctx:
        keep = ctx.enter_context(tc.tile_pool(name="keep", bufs=1))
        reuse = ctx.enter_context(tc.tile_pool(name="reuse", bufs=1))
        psum = ctx.enter_context(tc.psum_pool(name="psum", bufs=8))

        def sb(shape, dtype, name, tag=None):
            return keep.tile(shape, dtype, name=name, tag=tag or name, align_bytes=64)

        def load_list(src, name):
            tile = sb([P, src.shape[1]], U16, name)
            nc.sync.dma_start(tile[:], src)
            return tile

        def mx(acc, lhs, lhs_cols, rhs, rhs_cols):
            nc.tensor.matmul_mx(
                out=acc,
                lhsT=lhs[0][:, lhs_cols].bitcast(FP8X4),
                lhsT_scale=lhs[1][:, lhs_cols],
                rhs=rhs[0][:, rhs_cols].bitcast(FP8X4),
                rhs_scale=rhs[1][:, rhs_cols],
                start=True,
                stop=True,
            )

        def quantize(src, cols, name, at=None):
            if at is None:
                codes = sb([P, cols], U32, name + "_codes")
            else:
                codes = reuse.tile([P, cols], U32, name=name + "_codes", align_bytes=64, offset=at)
            scales = sb([P, cols], U8, name + "_scales")
            nc.vector.quantize_mx(out=codes[:].bitcast(FP8X4), scales=scales[:], in_=src)
            return codes, scales

        table_scales = sb([P, T], U8, "table_scales")
        nc.vector.memset(table_scales[:].bitcast(I32), 0)
        warm = sb([P, 2], F32, "warm")
        nc.vector.memset(warm[:, 0:1], 0.0)
        nc.scalar.activation(warm[:, 1:2], warm[:, 0:1], ACT.Relu)
        offs_t = load_list(offs, "offs_t")
        two_t = load_list(two, "two_t")
        w1_raw = sb([P, PACK, H], F32, "w1_raw")
        w1_v = w1.rearrange("(p j) c -> p j c", j=PACK)
        nc.sync.dma_start(w1_raw[:, 0:1, :], w1_v[:, 0:1, :])
        for q in range(4):
            nc.sync.dma_start(
                table_scales[q:P:32, :].bitcast(I32),
                x_scales[0, q:16:4, :].bitcast(I32),
            )
        nc.sync.dma_start(w1_raw[:, 1:4, :], w1_v[:, 1:4, :])
        table_words = sb([P, T], U32, "table_words")
        nc.sync.dma_start(
            table_words[:].bitcast(I32), x_words[0].rearrange("p n t -> p (n t)").bitcast(I32)
        )
        la_t = load_list(la, "la_t")
        lb_t = load_list(lb, "lb_t")
        w2_raw = reuse.tile([P, PACK, H], F32, name="w2_raw", align_bytes=64, offset=0)
        nc.sync.dma_start(w2_raw[:], w2.rearrange("(p j) c -> p j c", j=PACK))
        ga_t = sb([P, PACK], F32, "ga_t")
        nc.sync.dma_start(ga_t[:], ga.rearrange("(p t) o -> p (t o)", t=PACK))
        gb_t = sb([P, PACK], F32, "gb_t")
        nc.sync.dma_start(gb_t[:], gb.rearrange("(p t) o -> p (t o)", t=PACK))
        nq_t = load_list(nq, "nq_t")

        def cast_pair(raw, u, name, copy=nc.scalar.copy):
            grouped = sb([P, 2, P, PACK], BF16, name)
            copy(
                grouped[:].rearrange("p t m j -> p m j t"),
                raw[:].rearrange("p j (m t) -> p m j t", t=PACK)[:, :, :, 2 * u : 2 * u + 2],
            )
            return grouped

        xa_scales = sb([P, S], U8, "xa_scales")
        xb_scales = sb([P, V], U8, "xb_scales")
        xa_words = sb([P, S], U32, "xa_words")
        xb_words = sb([P, V], U32, "xb_words")
        nc.vector.tensor_copy(xa_scales[:], table_scales[:].indirect(offs_t[:]))
        nc.vector.tensor_copy(xb_scales[:], table_scales[:].indirect(two_t[:]))
        w1_bf = [cast_pair(w1_raw, u, "w1_bf%d" % u) for u in range(2)]
        w1_q = [
            quantize(w1_bf[0][:, t].rearrange("p m j -> p (m j)"), P, "w1_%d" % t, CODES_AT if t == 0 else None)
            for t in range(2)
        ]
        half = S // 2
        for h in range(2):
            nc.vector.tensor_copy(
                xa_words[:, h * half : (h + 1) * half],
                table_words[:].indirect(offs_t[:, h * half // PER_COL : (h + 1) * half // PER_COL]),
            )
        xa = (xa_words, xa_scales)
        xb = (xb_words, xb_scales)

        a_rows = []
        for t in range(PACK):
            rows = sb([P, S], F32, "a%d" % t)
            if t == 2:
                nc.vector.tensor_copy(xb_words[:], table_words[:].indirect(two_t[:]))
                w1_q.append(quantize(w1_bf[1][:].rearrange("p t m j -> p (t m j)"), 2 * P, "w1_23", CODES_AT))
            cols = slice(P, 2 * P) if t == 3 else slice(0, P)
            pieces = 2 if t == 0 else 1
            width = S // pieces
            for h in range(pieces):
                acc = psum.tile([P, width], F32, name="acc", tag="bank")
                span = slice(h * width, (h + 1) * width)
                mx(acc[:], w1_q[min(t, 2)], cols, xa, span)
                nc.scalar.copy(rows[:, span], acc[:])
            a_rows.append(rows)

        w2_bf = sb([P, PACK, P, PACK], BF16, "w2_bf")
        nc.scalar.copy(
            w2_bf[:].rearrange("p t m j -> p m j t"),
            w2_raw[:].rearrange("p j (m t) -> p m j t", t=PACK),
        )

        z_bf = reuse.tile([P, S, PACK], BF16, name="z_bf", align_bytes=64, offset=0)
        sorted_rows = []

        def order_pairs(t, pair):
            pq = pair[:, t % 2]
            nc.vector.tensor_copy(pq[:, 0, :], a_rows[t][:].indirect(la_t[:]))
            nc.vector.tensor_copy(pq[:, 1, :], a_rows[t][:].indirect(lb_t[:]))
            if t < 2:
                hi = sb([P, W], F32, "hi%d" % t)
                lo = sb([P, W], F32, "lo%d" % t)
            else:
                hi = reuse.tile([P, W], F32, name="hi%d" % t, align_bytes=64, offset=HI_AT[t])
                lo = reuse.tile([P, W], F32, name="lo%d" % t, align_bytes=64, offset=LO_AT[t])
            nc.vector.tensor_tensor(hi[:], pq[:, 0, :], pq[:, 1, :], ALU.max)
            nc.vector.tensor_tensor(lo[:], pq[:, 0, :], pq[:, 1, :], ALU.min)
            d = sb([P, S], F32, "d%d" % t)
            nc.vector.tensor_copy(d[:].indirect(la_t[:]), hi[:])
            nc.vector.tensor_copy(d[:].indirect(lb_t[:]), lo[:])
            sorted_rows.append(d)

        def weave_z(t):
            pieces = 2 if t == PACK - 1 else 1
            for h in range(pieces):
                span = slice(h * S // pieces, (h + 1) * S // pieces)
                nc.scalar.activation(
                    z_bf[:, span, t], sorted_rows[t][:, span], ACT.Copy, scale=ga_t[:, t : t + 1]
                )

        pq01 = sb([P, 2, 2, W], F32, "pq01")
        order_pairs(0, pq01)
        weave_z(0)
        order_pairs(1, pq01)
        w2_q = quantize(w2_bf[:].rearrange("p t m j -> p (t m j)"), H, "w2")
        weave_z(1)
        b_rows = []
        for t in range(PACK):
            rows = sb([P, V], F32, "b%d" % t)
            acc = psum.tile([P, V], F32, name="acc", tag="bank")
            mx(acc[:], w2_q, slice(t * P, (t + 1) * P), xb, slice(0, V))
            nc.scalar.activation(rows[:], acc[:], ACT.Copy, scale=gb_t[:, t : t + 1])
            b_rows.append(rows)
        pq23 = sb([P, 2, 2, W], F32, "pq23")
        order_pairs(2, pq23)
        weave_z(2)
        order_pairs(3, pq23)
        weave_z(3)

        out_v = out.rearrange("(m p) v -> p m v", p=P)
        starts = [sum(CHUNKS[:c]) for c in range(len(CHUNKS))]
        z2_bf = []

        def fetch(c):
            n = CHUNKS[c]
            if c == 1:
                planes = sb([P, PACK, n], BF16, "planes1", "d3")
            else:
                planes = reuse.tile([P, PACK, n], BF16, name="planes%d" % c, align_bytes=64, offset=LO_AT[2])
            lst = nq_t[:, starts[c] // PER_COL : (starts[c] + n) // PER_COL]
            for t in range(PACK):
                nc.vector.tensor_copy(planes[:, t, :], b_rows[t][:].indirect(lst))
            woven = sb([P, n, PACK], BF16, "z2_bf%d" % c)
            src = planes[:].rearrange("p t n -> p n t")
            if c == len(CHUNKS) - 1:
                nc.vector.tensor_copy(woven[:], src)
            else:
                nc.scalar.copy(woven[:], src)
            z2_bf.append(woven)

        def finish(c, z_q):
            n = CHUNKS[c]
            z2_q = quantize(z2_bf[c][:].rearrange("p n t -> p (n t)"), n, "z2_%d" % c)
            last = c == len(CHUNKS) - 1
            per_bank = 2 if (last or n == 256) else 4
            for g in range(PACK // per_bank):
                acc = psum.tile([P, per_bank, n], F32, name="acc", tag="bank")
                for i in range(per_bank):
                    m = g * per_bank + i
                    mx(acc[:, i, :], z_q[m // 2], slice(m % 2 * P, (m % 2 + 1) * P), z2_q, slice(0, n))
                res = sb([P, per_bank, n], F32, "res%d_%d" % (c, g))
                if last:
                    nc.vector.tensor_scalar(res[:], acc[:], 0.0625, 0.0, ALU.mult, ALU.max)
                else:
                    nc.scalar.activation(res[:], acc[:], ACT.Relu, scale=0.0625)
                queue = nc.scalar if c == 1 else nc.sync
                queue.dma_start(
                    out_v[:, g * per_bank : (g + 1) * per_bank, starts[c] : starts[c] + n], res[:]
                )

        fetch(0)
        z_q = [
            quantize(z_bf[:, h * half : (h + 1) * half, :].rearrange("p n t -> p (n t)"), half, "z_%d" % h)
            for h in range(2)
        ]
        fetch(1)
        finish(0, z_q)
        fetch(2)
        finish(1, z_q)
        finish(2, z_q)
